import numpy as np, ml_dtypes
CORES = [3,11,19,27,35,43,51,59]
N = 8
BF = ml_dtypes.bfloat16
V, G, H, RO = 2560, 256, 3, 4
W = V + H * G
LIM = 2 ** 19 - 1
def pack(v, p):
    return {"x": np.ascontiguousarray(v.reshape(N, 128, V)).astype(np.int32), "pt": np.ascontiguousarray(p).astype(np.int32)}
def signs(rng, *shape):
    return rng.choice(np.array([-1, 1]), shape)
def points(rng):
    return np.ascontiguousarray(np.argsort(rng.random((N, 8, W)), axis=-1)[..., :V])
def crowd(rng, quiet):
    pool = np.broadcast_to(rng.integers(-2 ** 16, 2 ** 16 + 1, (8, 16, 24)), (N, 8, 16, 24))
    near = np.take_along_axis(pool, rng.integers(0, 24, (N, 8, 1, V)), 3) * rng.choice(np.array([-3, -2, -1, 1, 2, 3]), (N, 8, 1, V))
    noise = np.exp2(2 + 15 * rng.random((N, 8, 1, V))) * rng.standard_normal((N, 8, 16, V), dtype=np.float32)
    loud = near * (rng.random((N, 8, 1, V)) < 0.5) + noise.astype(np.int64)
    dense = rng.choice(np.array([0.15, 0.3, 1.0]), (N, 8, 1, 1))
    calm = rng.integers(-LIM, LIM + 1, (N, 8, 16, V)) * (rng.random((N, 8, 16, V)) < dense)
    v = np.where(rng.random((N, 8, 1, V)) < quiet, calm, loud)
    return np.minimum(np.maximum(v, -LIM), LIM)
def setup_inputs(rng):
    quiet = rng.permuted(np.tile(np.array([0.0, 0.1, 0.3, 0.5, 0.7, 0.9, 0.95, 1.0]), (N, 1)), axis=1).reshape(N, 8, 1, 1)
    rest = rng.permuted(np.tile(np.array([0.0, 0.0, 0.0, 0.0, 0.3, 0.6, 0.8, 0.92]), (N, 1)), axis=1).reshape(N, 8, 1)
    v = crowd(rng, quiet) * (rng.random((N, 8, 1, V)) > 0.03); p = points(rng)
    p = np.where(rng.random((N, 8, V)) < rest, np.arange(V), p)
    o = np.argsort(rng.random((N, 8, V)), axis=-1); t = V // 16; i = o[..., :t]; s = o[..., t:2 * t]
    np.put_along_axis(v, i[:, :, None, :], np.take_along_axis(v, s[:, :, None, :], 3) * signs(rng, N, 8, 1, t), 3)
    np.put_along_axis(p, i, s, 2)
    return pack(v, p)
def setup_inputs_room(rng):
    v = signs(rng, N, 8, 16, V) * rng.integers(4, 1001, (N, 8, 16, V)); p = np.zeros((N, 8, V), np.int64)
    for q in range(N):
        for g in range(8):
            o = rng.permutation(V); a, b, z, m = o[:32], o[32:64], o[64:320], o[320:]
            v[q, g][:, b] = signs(rng, 16, 32) * rng.integers(5000, LIM + 1, (16, 32))
            v[q, g][:, o[64:320]] = 0; v[q, g][:, a] = 0
            v[q, g][rng.integers(0, 16, 32), a] = signs(rng, 32) * rng.integers(1, 4, 32)
            u = rng.random(V)
            w = np.where(u < 0.5, z[rng.integers(0, 256, V)], np.where(u < 0.75, b[rng.integers(0, 32, V)], np.arange(V)))
            w[b] = np.where(rng.random(32) < 0.5, b, z[rng.integers(0, 256, 32)])
            w[z] = rng.integers(V, W, 256)
            w[z[:H]] = V + np.arange(H) * G + G - 1; w[z[H:2 * H]] = V + np.arange(H) * G; w[a[:2 * H]] = z[:2 * H]
            n = int(rng.choice(np.array([0, 1, G - 1, G, G + 1, V - 320])))
            if q == 0: n = (G, G + 1, V - 320, G - 1, 1, 0, G, G + 1)[g]
            w[rng.permutation(m)[:n]] = a[rng.integers(0, 32, n)]
            p[q, g] = w
    return pack(v, p)
def setup_inputs_ties(rng):
    v = np.zeros((N, 8, 16, V), np.int64); p = np.zeros((N, 8, V), np.int64); h = (V - 2) // 2
    alt = np.where(np.arange(16) % 2 == 0, 1, -1)[:, None]
    for q in range(N):
        for g in range(8):
            o = rng.permutation(V); s, i = o[2:2 + h], o[2 + h:2 + 2 * h]
            y = np.repeat(2 * np.exp2(17 * rng.random((8, h))).astype(np.int64), 2, axis=0) * signs(rng, 16, h)
            one = np.zeros((16, h), np.int64); one[rng.integers(0, 16, h), np.arange(h)] = signs(rng, h)
            big = signs(rng, 16, h) * rng.integers(1, LIM + 1, (16, h)); sg = signs(rng, h); k = rng.integers(0, 7, h)
            kinds = np.stack([y * sg, (y >> 1) * sg, y * sg + one, y * alt * sg, big, 0 * y, big])
            v[q, g, int(rng.integers(0, 16)), o[0]] = 1
            v[q, g][:, s] = y; v[q, g][:, i] = kinds[k, :, np.arange(h)].T
            p[q, g, o[:2]] = rng.integers(0, W, 2)
            p[q, g, s] = rng.integers(0, W, h) if g % 2 == 0 else rng.choice(np.array([0, V - 1, V, W - 1]), h)
            p[q, g, i] = np.where(k == 4, o[0], np.where(k == 6, o[1], s))
    return pack(v, p)
def setup_inputs_still(rng):
    v = crowd(rng, np.zeros((N, 8, 1, 1)))
    lone = np.where(np.arange(16)[:, None] == rng.integers(0, 16, (N, 8, 1, V)), rng.integers(1, LIM + 1, (1, 8, 1, 1)) * signs(rng, N, 8, 1, V), 0)
    mask = np.zeros((N, 8, 1, 1), bool); q = int(rng.integers(0, N)); mask[q] = True; mask[:, int(rng.integers(0, 8))] = True
    own = np.argsort(rng.random((N, 8, V)), axis=-1)
    p = np.where(rng.random((N, 8, V)) < 0.5, rng.integers(V, W, (N, 8, V)), own); p[q] = own[q]
    return pack(np.where(mask, lone, v), p)
def setup_inputs_spread(rng):
    v = (np.exp2(19 * rng.random((N, 8, 1, V))) * np.exp2(-4 * rng.random((N, 8, 16, 1))) * (2 * rng.random((N, 8, 16, V)) - 1)).astype(np.int64)
    v = np.where(rng.random((N, 8, 1, V)) < 0.05, LIM * signs(rng, N, 8, 16, V), v) * (rng.random((N, 8, 1, V)) > 0.0625)
    p = points(rng); odd = (np.arange(8) % 2 == 1)[None, :, None]
    few = np.minimum((W * rng.random((N, 8, V)) ** 4).astype(np.int64), W - 1); few = np.where(rng.random((N, 8, V)) < 0.5, few, W - 1 - few)
    return pack(v, np.where(odd, few, p))
def small(rng, n):
    return signs(rng, 16, n) * rng.integers(1, 1001, (16, n))
def long(rng, n):
    return signs(rng, 16, n) * rng.integers(5000, LIM - 999, (16, n))
def stops(rng, v, p, red):
    o = rng.permutation(np.setdiff1d(np.arange(V), red)); y, w, z = o[:24], o[24:48], o[48:120].reshape(3, 24)
    base = long(rng, 24); i = np.concatenate([rng.integers(0, 24, len(red)), np.arange(24)]); m = np.concatenate([red, w])
    v[:, y] = base; v[:, m] = base[:, i] * signs(rng, len(m)) + small(rng, len(m))
    p[y] = y; p[red] = y[i[:len(red)]]; p[w] = z[0]; p[z[0]] = z[1]; p[z[1]] = z[2]; p[z[2]] = y
def far(rng, v, p):
    base = long(rng, 24); kk = rng.integers(0, 24, (N, G)); at = rng.integers(V, W, (N, V))
    kind = kk[(np.arange(N)[:, None] - (at - V) // G - 1) % N, (at - V) % G]
    for q in range(N):
        v[q] = base[:, kind[q]] * signs(rng, V) + small(rng, V)
        v[q][:, :G] = base[:, kk[q]] * signs(rng, G)
        p[q] = at[q]
def one(rng, v, p):
    base = long(rng, 1); j = rng.integers(0, G, N); turn = int(rng.integers(0, 2))
    for q in range(N):
        d = int(rng.integers(1, H + 1))
        v[q] = base * signs(rng, V) + small(rng, V)
        v[q][:, j[q]] = base[:, 0] * int(signs(rng, 1)[0])
        p[q] = j[q] if (q + turn) % 2 == 0 else V + (d - 1) * G + j[(q - d) % N]
        p[q, j[q]] = j[q]
def grow(rng, v, p):
    o = rng.permutation(16); u = int(rng.integers(480000, LIM - 199)); form = np.zeros((16, 3), np.int64)
    form[o[0]] = (u, u, 3 * u // 4); form[o[1:4]] = (-u, u, -(u // 2)); form[o[4:]] = (u, -(u // 3), 0)
    for q in range(N):
        m = rng.permutation(V); y, s, x, w, z = m[:24], m[24:48], m[48:120], m[120:168], m[168:312].reshape(3, 48)
        for k, i in ((0, x), (0, w), (1, y), (2, s)):
            v[q][:, i] = (form[:, k:k + 1] + rng.integers(-200, 201, (16, len(i)))) * signs(rng, len(i))
        p[q, x] = y[rng.integers(0, 24, 72)]; p[q, y] = s[rng.integers(0, 24, 24)]; p[q, s] = s
        p[q, w] = z[0]; p[q, z[0]] = z[1]; p[q, z[1]] = z[2]; p[q, z[2]] = V + rng.integers(0, H, 48) * G + rng.integers(0, 96, 48)
def setup_inputs_full(rng):
    v = np.zeros((N, 8, 16, V), np.int64); p = points(rng); kind = rng.permutation(np.array([0, 1, 2, 3, 4, 0, 1, 4]))
    for g in range(8):
        if kind[g] == 2: far(rng, v[:, g], p[:, g])
        elif kind[g] == 3: one(rng, v[:, g], p[:, g])
        elif kind[g] == 4: grow(rng, v[:, g], p[:, g])
        else:
            for q in range(N):
                red = np.arange(int(rng.integers(0, 16)), V, 16) if kind[g] == 0 else 256 * int(rng.integers(1, V // 256)) + np.arange(256)
                stops(rng, v[q, g], p[q, g], red)
    return pack(v, p)
def check_inputs(d):
    bad = []
    for k, lo, hi in (("x", -LIM, LIM), ("pt", 0, W - 1)):
        if np.min(d[k]) < lo or np.max(d[k]) > hi: bad.append("range of " + k)
    return bad
def reference(x, pt):
    v = x.astype(np.int64).reshape(N, 8, 16, V); p = pt.astype(np.int64)
    num = np.broadcast_to(np.arange(G), (N, 8, G)); gv = v[..., :G]
    for rnd in range(RO):
        w = np.concatenate([v] + [np.roll(gv, d, axis=0) for d in range(1, H + 1)], axis=3)
        ptr = np.concatenate([p] + [np.roll(num, d, axis=0) for d in range(1, H + 1)], axis=2)
        y = np.take_along_axis(w, p[:, :, None, :], 3)
        old = np.sum(np.abs(v), axis=2); lp = np.sum(np.abs(v + y), axis=2); lm = np.sum(np.abs(v - y), axis=2)
        plus = (lp > 0) & (lp < old); minus = (lm > 0) & (lm < old)
        v = np.where(plus[:, :, None, :], v + y, np.where(minus[:, :, None, :], v - y, v))
        done = plus | minus
        p = np.where(done, p, np.take_along_axis(ptr, p, 2))
        num = np.argsort(np.where(done, 0, 1), axis=2, kind="stable")[..., :G]
        gv = np.take_along_axis(v, num[:, :, None, :], 3)
    return {"yx": v.reshape(N, 128, V).astype(np.float32), "yc": p.astype(np.float32)}

from concourse.bass import DstId, RemoteDMATransfer
from concourse.mybir import AluOpType as A, ActivationFunctionType as AF

V, G, H, RO = 2560, 256, 3, 4
GW = H * G
WW = GW + V + G
RW = WW + 2 * V
CH = ((0, 512), (512, 1024), (1536, 1024))
NC = 176
F, B, I, U, HF = "float32", "bfloat16", "int32", "uint16", "float16"


def sb(n, d):
    return ("sbuf", [128] + (n if isinstance(n, list) else [n]), d)


SCRATCH = {
    "big": sb(RO * RW, F), "ab": sb(2 * V, F), "xi": sb(V, I), "tb0": sb(GW + V, B), "tb1": sb(GW + V, B),
    "nt": sb(V + G, B), "sc": sb(2992, F), "snd": sb(3 * G, F), "goff": sb(48, U), "nrc": sb(144, U),
    "ptq": sb(160, I), "e1": sb(160, F), "e2": sb(160, F), "e3": sb(160, F), "hi": sb(160, B), "lo": sb(160, B),
    "j1": sb(160, F), "j2": sb(160, F), "jhi": sb(160, B), "jlo": sb(160, B),
    "off": sb(160, U), "off2": sb(160, U), "off3": sb(160, U), "soff": sb(12, U),
    "pe": sb(160, F), "jp": sb(160, F), "jp0": sb(160, F), "je": sb(160, F), "o1": sb(160, F), "o2": sb(160, F),
    "lx": sb(384, F), "lt": sb(384, F), "ld": sb(384, F), "uu": sb(384, F), "ff": sb(384, B), "tc": sb(256, F),
    "rs": sb([NC, 2], B), "crs": sb([NC, 2], B), "r0": sb([NC, 2], B), "r1": sb([NC, 2], B), "r2": sb([NC, 2], B),
    "dd": sb(NC, F), "dc": sb(NC, F), "s0": sb(24, F), "s1": sb(24, F), "inc": sb(G, F), "qq": sb(G, HF),
    "cidx": sb(NC, F), "pci": sb(8, I), "pcf": sb(8, F), "mb": sb(144, B), "mh": sb(144, HF), "bi": sb(8, F),
    "tri": sb(128, B), "tra": sb(128, B), "trb": sb(128, B), "idn": sb(128, B), "d64": sb(128, F), "d32": sb(64, F),
    "w64": sb(64, B), "w32": sb(32, B), "c16": sb(160, B), "m768": sb(160, B),
    "one": sb(160, B), "onf": sb(64, F), "neg": sb(160, B), "pos": sb(16, B), "wp": sb(64, B), "wm": sb(64, B),
    "y1": sb(160, F), "y2": sb(160, F),
    "px": ("psum", [128, V], F), "pa": ("psum", [128, 512], F), "pb": ("psum", [128, 512], F), "pc": ("psum", [128, 512], F),
}
SEMAPHORES = (["cv", "cs", "ct", "cg", "sent", "lp", "th", "tl", "n0", "n1", "n2", "n3", "n4", "n5", "oc"]
              + ["lx%d" % k for k in range(6)] + ["ox%d" % k for k in range(5)] + ["xc%d" % k for k in range(15)]
              + ["arr%d" % k for k in range(RO)] + ["num%d" % k for k in range(1, RO)])
PSUM = ("px", "pa", "pb", "pc")


def rank_program(g, core, T, topo):
    rank = T.rank_of(core)
    if rank is None:
        return
    n = len(T.cores)
    Q = {"v": g.vector, "s": g.scalar, "t": g.tensor, "g": g, "y": g.sync}
    own = {"v": "cv", "s": "cs", "t": "ct", "g": "cg"}
    total = {}
    waited = {}
    hist = {}

    def need(q, rd, wr):
        deps = {}
        for acc, w in ((rd, False), (wr, True)):
            for (name, lo, hi) in acc:
                for (l2, h2, w2, q2, sem, val) in hist.get(name, []):
                    hit = l2 < hi and lo < h2 and (w or w2)
                    if name in PSUM:
                        if q2 != q:
                            hit = l2 // 512 <= (hi - 1) // 512 and lo // 512 <= (h2 - 1) // 512
                        elif q == "t":
                            hit = False
                    if hit and deps.get(sem, 0) < val:
                        deps[sem] = val
        for sem, val in deps.items():
            if waited.get((q, sem), 0) < val:
                Q[q].wait_ge(T.sem[sem], val)
                waited[(q, sem)] = val

    def note(q, rd, wr, sem, val):
        for acc, w in ((rd, False), (wr, True)):
            for (name, lo, hi) in acc:
                h = hist.setdefault(name, [])
                if w:
                    h[:] = [e for e in h if not (lo <= e[0] and e[1] <= hi)]
                h.append([lo, hi, w, q, sem, val])

    def drain(q):
        sem = own[q]
        if waited.get((q, sem), 0) < total.get(sem, 0):
            Q[q].wait_ge(T.sem[sem], total[sem])
            waited[(q, sem)] = total[sem]

    def op(q, call, rd, wr):
        need(q, rd, wr)
        sem = own[q]
        if q == "g":
            drain(q)
        call().then_inc(T.sem[sem], 1)
        total[sem] = total.get(sem, 0) + 1
        note(q, rd, wr, sem, total[sem])

    def dma(q, out, in_, rd, wr, sem):
        need(q, rd, wr)
        Q[q].dma_start(out, in_).then_inc(T.sem[sem], 16)
        total[sem] = total.get(sem, 0) + 16
        note("d" + sem, rd, wr, sem, total[sem])

    def dmas(items, wr):
        before = list(hist[wr[0]])
        mine = []
        for (out, in_, rd, sem) in items:
            hist[wr[0]][:] = before
            dma("y", out, in_, rd, [wr], sem)
            mine.append(hist[wr[0]][-1])
        hist[wr[0]][:] = hist[wr[0]][:-1] + mine

    def R(name, lo=0, hi=1 << 20):
        return (name, lo, hi)

    def ap(r, p0=0, p1=128):
        return T[r[0]][p0:p1, r[1]:r[2]]

    def ts(out, in0, s1, s2, o0, o1, rd, wr):
        if s2 is None:
            op("v", lambda: g.vector.tensor_scalar(out, in0, s1, None, o0), rd, wr)
        else:
            op("v", lambda: g.vector.tensor_scalar(out, in0, s1, s2, o0, o1), rd, wr)

    def tt(out, in0, in1, o, rd, wr):
        op("v", lambda: g.vector.tensor_tensor(out, in0, in1, o), rd, wr)

    def cp(out, in_, rd, wr):
        op("v", lambda: g.vector.tensor_copy(out, in_), rd, wr)

    def ms(out, val, wr):
        op("v", lambda: g.vector.memset(out, val), [], wr)

    def scan(out, d0, d1, rd, wr):
        op("v", lambda: g.vector.tensor_tensor_scan(out, d0, d1, 0.0, A.add, A.max), rd, wr)

    def act(out, in_, f, rd, wr, scale=1.0):
        if scale == 1.0:
            op("s", lambda: g.scalar.activation(out, in_, f), rd, wr)
        else:
            op("s", lambda: g.scalar.activation(out, in_, f, scale=scale), rd, wr)

    def mm(out, lhsT, rhs, start, stop, rd, wr):
        op("t", lambda: g.tensor.matmul(out, lhsT, rhs, start, stop), rd, wr)

    def iota(out, pat, base, cm, wr, flt=True):
        if flt:
            op("g", lambda: g.iota(out, pat, base, cm, allow_small_or_imprecise_dtypes=True), [], wr)
        else:
            op("g", lambda: g.iota(out, pat, base, cm), [], wr)

    def sel(out, in_, pat, cmp, base, cm, rd, wr):
        op("g", lambda: g.affine_select(out, in_, pat, cmp, 0.0, base, cm), rd, wr)

    peers = [T.cores[(rank + d) % n] for d in range(1, H + 1)]
    emask = topo.mask(core, peers[0])
    for c in peers[1:]:
        emask = emask & topo.mask(core, c)
    neng = bin(emask).count("1")
    ids = [DstId(rid=topo.addr(c)[0], pnc=topo.addr(c)[1]) for c in peers]

    def send(src, dsts, sem):
        need("g", [src], [])
        g.remote_dma_fused([RemoteDMATransfer(dst_ids=ids, dma_engine_mask=emask, remote_sem=T.sem[sem], srcs=[ap(src)],
                                              dsts=[ap(r) for r in dsts])], local_sem=T.sem.sent)
        total["sent"] = total.get("sent", 0) + neng
        total[sem] = H * neng
        note("remote", [], dsts, sem, H * neng)

    def X(r, a=0, b=V):
        return R("big", r * RW + GW + a, r * RW + GW + b)

    def X2(r, a, b):
        return R("xi", a, b) if r == 0 else R("big", (r + 2) % RO * RW + WW + a, (r + 2) % RO * RW + WW + b)

    def gather(q, out, win, offs):
        src = ap(win).indirect(ap(offs))
        if q == "v":
            cp(ap(out), src, [win, offs], [out])
        else:
            act(ap(out), src, AF.Copy, [win, offs], [out])

    TB = ("tb0", "tb1")
    pi, pcol, g15 = T.pcf[:, 0:1], T.pcf[:, 1:2], T.pcf[:, 2:3]
    PC = R("pcf", 0, 3)

    def S_b(i):
        return T.mb[:, 15 - i:143 - i]

    def dup(nm, nc):
        for h in range(2):
            for hh in range(2):
                sel(T[nm][nc * h:nc * h + nc, nc * hh:nc * hh + nc], T.onf[nc * h:nc * h + nc, 0:nc], [[-1, nc]], A.is_equal, 0, 1,
                    [R("onf")], [R(nm, 2 * hh + h, 2 * hh + h + 1)])

    cuts = (0, 256, 512, 1024, 1536, 2048, 2560)
    dma("y", T.xi[:, 0:256], T.x[:, 0:256], [], [R("xi", 0, 256)], "lx0")
    dma("y", T.ptq[:], T.pt[:], [], [R("ptq")], "lp")
    for k in range(1, 6):
        a, b = cuts[k], cuts[k + 1]
        dma("y", T.xi[:, a:b], T.x[:, a:b], [], [R("xi", a, b)], "lx%d" % k)

    iota(T.pci[:, 0:1], [[0, 1]], 0, 1, [R("pci", 0, 1)], False)
    iota(T.cidx[:], [[1, NC]], 0, 0, [R("cidx")])
    iota(T.onf[:], [[0, 64]], 1, 0, [R("onf")])
    dup("d32", 32)
    ms(T.tb0[:, GW:], 0.0, [R("tb0", GW, GW + V)])
    ts(T.pci[:, 4:5], T.pci[:, 0:1], 15, None, A.bitwise_and, None, [R("pci", 0, 1)], [R("pci", 4, 5)])
    cp(pcol, T.pci[:, 0:1], [R("pci", 0, 1)], [R("pcf", 1, 2)])
    cp(pi, T.pci[:, 4:5], [R("pci", 4, 5)], [R("pcf", 0, 1)])
    ts(g15, pcol, pi, 15.0, A.subtract, A.add, [R("pcf", 0, 2)], [R("pcf", 2, 3)])
    ts(T.bi[:], T.cidx[:, 15:128:16], g15, None, A.is_equal, None, [R("cidx"), PC], [R("bi")])
    ts(T.mb[:], T.cidx[:, 0:144], g15, None, A.is_equal, None, [R("cidx"), PC], [R("mb")])

    def conv(k):
        a, b = cuts[k], cuts[k + 1]
        cp(ap(X(0, a, b)), T.xi[:, a:b], [R("xi", a, b)], [X(0, a, b)])

    conv(0)
    send(X(0, 0, G), [R("big", d * G, (d + 1) * G) for d in range(H)], "arr0")
    ts(T.e1[:], T.ptq[:], 2559.5, -float(V + GW), A.is_gt, A.mult, [R("ptq")], [R("e1")])
    ts(T.e2[:], T.ptq[:], float(GW), None, A.add, None, [R("ptq")], [R("e2")])
    tt(T.e3[:], T.e1[:], T.e2[:], A.add, [R("e1"), R("e2")], [R("e3")])
    cp(T.hi[:], T.e3[:], [R("e3")], [R("hi")])
    tt(T.lo[:], T.e3[:], T.hi[:], A.subtract, [R("e3"), R("hi")], [R("lo")])
    dmas([(T.tb0[0:128:16, GW:], T.hi[:], [R("hi")], "th"), (T.tb0[1:128:16, GW:], T.lo[:], [R("lo")], "tl")], R("tb0", GW, GW + V))
    conv(1)
    conv(2)
    ts(T.mh[:], T.cidx[:, 0:144], g15, None, A.is_equal, None, [R("cidx"), PC], [R("mh")])
    ts(T.tra[:], T.cidx[:, 0:128], pcol, None, A.is_ge, None, [R("cidx"), PC], [R("tra")])
    ts(T.trb[:], T.cidx[:, 0:128], g15, 2.0 ** -18, A.is_le, A.mult, [R("cidx"), PC], [R("trb")])
    conv(3)
    ts(T.dc[:], T.cidx[:], 1024.5 + 1.0 / 128, None, A.add, None, [R("cidx")], [R("dc")])
    tt(T.tri[:], T.tra[:], T.trb[:], A.mult, [R("tra"), R("trb")], [R("tri")])
    ms(T.s0[:, 0:22:2], -1.0e6, [R("s0")])
    conv(4)
    ts(T.s0[:, 1:22:2], T.cidx[:, 0:NC:16], pi, float(V + G), A.add, A.add, [R("cidx"), PC], [R("s0")])
    ms(T.inc[:], 1.0 / 64, [R("inc")])
    ts(T.pcf[:, 3:4], pi, 160.0, None, A.mult, None, [PC], [R("pcf", 3, 4)])
    conv(5)

    iota(T.j1[:], [[1, 160]], GW, 0, [R("j1")])
    iota(T.c16[:], [[16, 160]], 0, 0, [R("c16")])
    dup("d64", 64)
    iota(T.one[:], [[0, 160]], 1, 0, [R("one")])
    iota(T.wp[:], [[0, 64]], V + G, 0, [R("wp")])
    iota(T.wm[:], [[0, 64]], 2 * V + G, 0, [R("wm")])
    sel(T.idn[:], T.one[:, 0:128], [[-1, 128]], A.is_equal, 0, 1, [R("one")], [R("idn")])
    for nm, nc in (("w32", 32), ("w64", 64)):
        for h, src in ((0, "wp"), (1, "wm")):
            sel(T[nm][nc * h:nc * h + nc, :], T[src][nc * h:nc * h + nc, 0:nc], [[-1, nc]], A.is_equal, 0, 1, [R(src)], [R(nm, h, h + 1)])
    iota(T.neg[:], [[0, 160]], -4096, 0, [R("neg")])
    iota(T.pos[:], [[0, 16]], 4096, 0, [R("pos")])
    iota(T.crs[:, 0:160, :], [[0, 160], [0, 2]], 0, 0, [R("crs", 0, 1)])
    iota(T.crs[:, 160:NC, 0], [[0, 16]], -4096, 0, [R("crs", 1, 2)])
    iota(T.crs[:, 160:NC, 1], [[1, 16]], 0, 0, [R("crs", 2, 3)])
    for q, (b0, ln) in enumerate(CH):
        nc, cb, nm = ln // 16, b0 // 16, "r%d" % q
        for h in range(2):
            p0, p1 = nc * h, nc * h + nc
            sel(T[nm][p0:p1, cb:160, 1], T.one[p0:p1, cb:160], [[1, 160 - cb]], A.is_gt, 0, -1, [R("one")], [R(nm, 4 * h, 4 * h + 1)])
            sel(T[nm][p0:p1, cb:160, 0], T.neg[p0:p1, cb:160], [[1, 160 - cb]], A.is_equal, 0, -1, [R("neg")], [R(nm, 4 * h + 1, 4 * h + 2)])
            if q == 0:
                sel(T[nm][p0:p1, 160:NC, 1], T.one[p0:p1, 0:16], [[-1, 16]], A.is_ge, 0, 1, [R("one")], [R(nm, 4 * h + 2, 4 * h + 3)])
                sel(T[nm][p0:p1, 160:NC, 0], T.pos[p0:p1, :], [[-1, 16]], A.is_equal, 0, 1, [R("pos")], [R(nm, 4 * h + 3, 4 * h + 4)])
        if q > 0:
            iota(T[nm][:, 160:NC, :], [[0, 16], [1, 2]], 0, 0, [R(nm, 8, 9)])
    iota(T.m768[:], [[0, 160]], -GW, 0, [R("m768")])

    def twice(r, k):
        a, b = 512 * k, 512 * k + 512
        act(T.px[:, a:b], ap(X(r, a, b)), AF.Copy, [X(r, a, b)], [R("px", a, b)], scale=2.0)

    def wrap(tb, c0, c1, ps):
        for i in range(16):
            mm(ap(ps), S_b(i), T[tb][:, GW + 16 * c0 + i:GW + 16 * c1:16], i == 0, i == 15,
               [R("mb"), R(tb, GW + 16 * c0, GW + 16 * c1)], [ps])

    def lists(c0, c1, ps):
        cp(T.off[:, c0:c1], ap(ps), [ps], [R("off", c0, c1)])

    def jump():
        cp(T.pe[:], T.off[:], [R("off")], [R("pe")])
        tt(T.jp0[:], T.pe[:], T.je[:], A.subtract, [R("pe"), R("je")], [R("jp0")])
        ts(T.jp[:], T.jp0[:], 1.0 / 4096, None, A.mult, None, [R("jp0")], [R("jp")])

    for k in range(5):
        a, b = 512 * k, 512 * k + 512
        act(T.ab[:, a:b], ap(X(0, a, b)), AF.Abs, [X(0, a, b)], [R("ab", a, b)])
        if k < 3:
            twice(0, k)
    twice(0, 3); twice(0, 4)
    for i in range(16):
        mm(T.pb[0:32, i:128:16], T.ab[:, i:512:16], T.bi[:], True, True, [R("ab", 0, 512), R("bi")], [R("pb", 0, 128)])
    wrap("tb0", 0, 160, R("pa", 0, 160))
    for i in range(16):
        mm(T.pc[:, i:128:16], T.ab[:, 512 + i:V:16], T.bi[:], True, True, [R("ab", 512, V), R("bi")], [R("pc", 0, 128)])
    ms(T.nt[:], 0.0, [R("nt")])
    ts(T.j2[:], T.j1[:], T.pcf[:, 3:4], None, A.add, None, [R("j1"), R("pcf", 3, 4)], [R("j2")])
    lists(0, 160, R("pa", 0, 160))
    cp(T.jhi[:], T.j2[:], [R("j2")], [R("jhi")])
    ts(T.je[:], T.c16[:], pi, float(GW), A.add, A.add, [R("c16"), PC], [R("je")])
    tt(T.jlo[:], T.j2[:], T.jhi[:], A.subtract, [R("j2"), R("jhi")], [R("jlo")])
    items = []
    for k, nm in enumerate(("jhi", "jlo")):
        items += [(T.nt[k:128:16, 0:V], T[nm][:], [R(nm)], "n%d" % (3 * k)),
                  (T.nt[k:128:16, V:V + 160], T[nm][0:128:16, :], [R(nm)], "n%d" % (3 * k + 1)),
                  (T.nt[k:128:16, V + 160:V + G], T[nm][1:128:16, 0:96], [R(nm)], "n%d" % (3 * k + 2))]
    dmas(items, R("nt"))
    act(ap(X(0, V, V + G)), ap(X(0, 0, G)), AF.Copy, [X(0, 0, G)], [X(0, V, V + G)])
    act(ap(X(1, V, V + G)), ap(X(0, 0, G)), AF.Copy, [X(0, 0, G)], [X(1, V, V + G)])
    act(T.tc[0:32, 0:128], T.pb[0:32, 0:128], AF.Copy, [R("pb", 0, 128)], [R("tc", 0, 128)])
    act(T.tc[:, 128:256], T.pc[:, 0:128], AF.Copy, [R("pc", 0, 128)], [R("tc", 128, 256)])
    mm(T.pc[0:64, 128:256], T.d32[0:32, :], T.tc[0:32, 0:128], True, True, [R("d32"), R("tc", 0, 128)], [R("pc", 128, 256)])
    drain("t")
    mm(T.pc[:, 256:384], T.d64[0:64, :], T.tc[0:64, 128:256], True, True, [R("d64"), R("tc", 128, 256)], [R("pc", 256, 384)])
    drain("t")
    mm(T.pc[:, 384:512], T.d64[64:128, :], T.tc[64:128, 128:256], True, True, [R("d64"), R("tc", 128, 256)], [R("pc", 384, 512)])

    TP = (R("pa", 0, 128), R("pa", 128, 256), R("pb", 0, 128))
    MS = (64, 128, 128)
    for r in range(RO):
        last = r == RO - 1
        base = r * RW
        win = R("big", base, base + GW + V)
        upw = R("big", base + GW, base + RW)
        tb, tn = TB[r % 2], TB[(r + 1) % 2]

        def S(a, b):
            return R("big", base + WW + a, base + WW + b)

        def abreg(k, h):
            b0, ln = CH[0 if k == 0 else (k + 1) // 2]
            o = 2 * b0 + h * ln + 512 * k - b0
            return R("ab", o, o + 512)

        def vs(k):
            a, b = 512 * k, 512 * k + 512
            o = R("off", 32 * k, 32 * k + 32)
            tt(ap(S(a, b)), ap(win).indirect(ap(o)), ap(X2(r, a, b)), A.add, [win, o, X2(r, a, b)], [S(a, b)])
            act(ap(abreg(k, 0)), ap(S(a, b)), AF.Abs, [S(a, b)], [abreg(k, 0)])

        def vd(k):
            a, b = 512 * k, 512 * k + 512
            tt(ap(S(V + a, V + b)), T.px[:, a:b], ap(S(a, b)), A.subtract, [R("px", a, b), S(a, b)], [S(V + a, V + b)])
            act(ap(abreg(k, 1)), ap(S(V + a, V + b)), AF.Abs, [S(V + a, V + b)], [abreg(k, 1)])

        def sums(q, i0=0, i1=16):
            b0, ln = CH[q]
            nm, lo, hi = TP[q]
            for i in range(i0, i1):
                mm(T[nm][0:MS[q], lo + i:hi:16], T.ab[:, 2 * b0 + i:2 * b0 + 2 * ln:16], T.bi[:], True, True,
                   [R("ab", 2 * b0, 2 * b0 + 2 * ln), R("bi")], [TP[q]])

        def verdict(q):
            m, c = MS[q], R("lx", 128 * q, 128 * q + 128)
            u, f = R("uu", c[1], c[2]), R("ff", c[1], c[2])
            tt(ap(u, 0, m), ap(TP[q], 0, m), ap(c, 0, m), A.is_lt, [TP[q], c], [u])
            tt(ap(f, 0, m), ap(TP[q], 0, m), ap(u, 0, m), A.min, [TP[q], u], [f])

        def code(q):
            b0, ln = CH[q]
            m, cb, nc = MS[q], b0 // 16, ln // 16
            o, f, w = R("pc", cb, cb + nc), R("ff", 128 * q, 128 * q + 128), ("w32" if q == 0 else "w64")
            mm(ap(o), T.idn[:], T.c16[:, cb:cb + nc], True, False, [R("idn"), R("c16")], [o])
            mm(ap(o), ap(f, 0, m), T[w][0:m, :], False, True, [f, R(w)], [o])
            if last:
                o2 = R("pc", 160 + cb, 160 + cb + nc)
                mm(ap(o2), ap(f, 0, m), T["r%d" % q][0:m, cb:cb + nc, 0], True, True, [f, R("r%d" % q)], [o2])

        def codeu(c0, c1):
            ts(T.off2[:, c0:c1], T.pc[:, c0:c1], pi, None, A.add, None, [R("pc", c0, c1), PC], [R("off2", c0, c1)])

        def gap(q):
            m, c = MS[q], R("lx", 128 * q, 128 * q + 128)
            tt(T.lt[0:m, c[1]:c[2]], ap(c, 0, m), ap(TP[q], 0, m), A.subtract, [c, TP[q]], [R("lt", c[1], c[2])])

        def drop(q):
            m, a, b = MS[q], 128 * q, 128 * q + 128
            tt(T.ld[0:m, a:b], T.lt[0:m, a:b], T.ff[0:m, a:b], A.mult, [R("lt", a, b), R("ff", a, b)], [R("ld", a, b)])

        def both(q):
            m, a, o = MS[q], 128 * q, R("pc", 256 + 128 * (q % 2), 384 + 128 * (q % 2))
            nm = "d32" if q == 0 else "d64"
            mm(ap(o, 0, m), T[nm][0:m, :], T.ld[0:m, a:a + 128], True, True, [R(nm), R("ld", a, a + 128)], [o])

        def shorter(q):
            m, c, o = MS[q], R("lx", 128 * q, 128 * q + 128), R("pc", 256 + 128 * (q % 2), 384 + 128 * (q % 2))
            tt(ap(c, 0, m), ap(c, 0, m), ap(o, 0, m), A.subtract, [c, o], [c])

        def ranks(c0, c1, q, start, stop):
            f, o = R("ff", 128 * q, 128 * q + 128), R("pa", 2 * c0, 2 * c1)
            mm(ap(o), ap(f, 0, MS[q]), T["r%d" % q][0:MS[q], c0:c1, :], start, stop, [f, R("r%d" % q)], [o])

        def ranked(c0, c1):
            o = R("pa", 2 * c0, 2 * c1)
            tt(T.rs[:, c0:c1, :], ap(o), T.crs[:, c0:c1, :], A.add, [o, R("crs")], [R("rs", 2 * c0, 2 * c1)])

        def update(q, k):
            a, b = 512 * k, 512 * k + 512
            out = X(0, a, b) if last else X(r + 1, a, b)
            gather(q, out, upw, R("off2", 32 * k, 32 * k + 32))
            if last:
                dma("y", T.yx[:, a:b], ap(out), [out], [], "ox%d" % k)
            else:
                dma("y", ap(X2(r + 1, a, b)), ap(out), [out], [X2(r + 1, a, b)], "xc%d" % (5 * r + k))

        def homes():
            if r == 0:
                for d in range(H):
                    act(T[tb][:, d * G:(d + 1) * G], T.nt[:, 0:G], AF.Copy, [R("nt")], [R(tb, d * G, (d + 1) * G)])
            else:
                gather("s", R(tb, 0, GW), R("nt", 0, V + G), R("nrc", 48 * (r - 1), 48 * r))

        def pointers(q, k):
            gather(q, R(tn, GW + 512 * k, GW + 512 * k + 512), R(tb, 0, GW + V), R("off3", 32 * k, 32 * k + 32))

        def third(c0, c1):
            tt(T.o2[:, c0:c1], T.o1[:, c0:c1], T.pe[:, c0:c1], A.add, [R("o1", c0, c1), R("pe", c0, c1)], [R("o2", c0, c1)])
            cp(T.off3[:, c0:c1], T.o2[:, c0:c1], [R("o2", c0, c1)], [R("off3", c0, c1)])

        vs(0); vd(0)
        if r == 0:
            act(T.lx[0:64, 0:128], T.pc[0:64, 128:256], AF.Copy, [R("pc", 128, 256)], [R("lx", 0, 128)])
            act(T.lx[:, 128:384], T.pc[:, 256:512], AF.Copy, [R("pc", 256, 512)], [R("lx", 128, 384)])
        sums(0)
        vs(1); vd(1); vs(2); vd(2); sums(1)
        vs(3); vd(3); vs(4); vd(4)
        verdict(0); verdict(1)
        if not last:
            gap(0); gap(1)
        sums(2, 0, 3); code(0); code(1); sums(2, 3, 10)
        codeu(0, 96)
        if not last:
            ranks(0, 96, 0, True, False); ranks(32, 96, 1, False, True)
            ranks(96, NC, 0, True, False); ranks(96, NC, 1, False, False)
            drop(0); drop(1)
            jump()
            ranked(0, 96)
            ms(T.sc[:, 0:G], 0.0, [R("sc")])
        sums(2, 10, 16)
        if last:
            update("s", 0); update("s", 1); update("v", 2)
            jump()
            verdict(2); code(2)
            tt(T.o1[:, 0:96], T.pc[:, 160:256], T.jp[:, 0:96], A.mult, [R("pc", 160, 256), R("jp")], [R("o1", 0, 96)])
            codeu(96, 160)
            tt(T.o1[:, 96:160], T.pc[:, 256:320], T.jp[:, 96:160], A.mult, [R("pc", 256, 320), R("jp")], [R("o1", 96, 160)])
            homes()
            update("s", 3); update("v", 4)
            third(0, 160)
            pointers("v", 0); pointers("s", 1); pointers("v", 2); pointers("s", 3); pointers("v", 4)
            o = R("pa", 0, 160)
            mm(ap(o), T.idn[:], T.m768[:], True, False, [R("idn"), R("m768")], [o])
            for q in range(16):
                c = R(tn, GW + 160 * q, GW + 160 * q + 160)
                mm(ap(o), S_b(q), ap(c), False, q == 15, [R("mb"), c], [o])
            ts(T.y1[:], ap(o), -0.5, float(V + GW), A.is_lt, A.mult, [o], [R("y1")])
            tt(T.y2[:], ap(o), T.y1[:], A.add, [o, R("y1")], [R("y2")])
            dma("s", T.yc[:], T.y2[:], [R("y2")], [], "oc")
            break
        both(0); both(1)
        update("s", 0); update("s", 1); update("s", 2)
        verdict(2)
        ranks(96, NC, 2, False, True)
        code(2)
        ranked(96, NC)
        codeu(96, 160)
        update("s", 3); update("s", 4)
        dp, wp_ = R("pb", 128, 128 + NC), R("pa", 352, 374)
        mm(ap(dp), T.tri[:], T.rs[:, :, 0], True, True, [R("tri"), R("rs")], [dp])
        for i in range(16):
            mm(ap(wp_), S_b(i), T.rs[:, i:NC:16, :], i == 0, i == 15, [R("mb"), R("rs")], [wp_])
        tt(T.dd[:], ap(dp), T.dc[:], A.add, [dp, R("dc")], [R("dd")])
        shorter(0); shorter(1)
        scan(T.s1[:, 0:22], T.s0[:, 0:22], ap(wp_), [R("s0"), wp_], [R("s1")])
        cp(T.soff[:, 0:11], T.s1[:, 1:22:2], [R("s1")], [R("soff")])
        cp(T.sc[:, 0:2992].indirect(T.soff[:, 0:11]), T.dd[:], [R("soff"), R("dd")], [R("sc")])
        scan(T.qq[:], T.inc[:], T.sc[:, 0:G], [R("inc"), R("sc")], [R("qq")])
        gp = R("pc", 160, 176)
        for i in range(16):
            mm(ap(gp), T.mh[:, 15 - i:143 - i], T.qq[:, i:G:16], i == 0, i == 15, [R("mh"), R("qq")], [gp])
        tt(T.o1[:], T.rs[:, 0:160, 0], T.jp[:], A.mult, [R("rs"), R("jp")], [R("o1")])
        gap(2)
        go = R("goff", 16 * r, 16 * r + 16)
        ts(ap(go), ap(gp), -16384.0, None, A.add, None, [gp], [go])
        sn = R("snd", G * r, G * r + G)
        gather("v", sn, X(r + 1, 0, V + G), go)
        send(sn, [R("big", base + RW + d * G, base + RW + (d + 1) * G) for d in range(H)], "arr%d" % (r + 1))
        send(go, [R("nrc", 48 * r + 16 * d, 48 * r + 16 * d + 16) for d in range(H)], "num%d" % (r + 1))
        homes()
        twice(r + 1, 0); twice(r + 1, 1)
        third(0, 160)
        pointers("v", 0); pointers("v", 1)
        wrap(tn, 0, 64, R("pa", 0, 64))
        pointers("v", 2); pointers("s", 3); pointers("s", 4)
        for k in range(2, 5):
            twice(r + 1, k)
        if r + 2 < RO:
            act(ap(X(r + 2, V, V + G)), ap(X(r + 1, 0, G)), AF.Copy, [X(r + 1, 0, G)], [X(r + 2, V, V + G)])
        wrap(tn, 64, 160, R("pb", 320, 416))
        lists(0, 64, R("pa", 0, 64))
        drop(2); both(2)
        lists(64, 160, R("pb", 320, 416))
        shorter(2)

    for sem, val in total.items():
        g.wait_ge(T.sem[sem], val)
